import numpy as np
import ml_dtypes


def mxq(x, axis, fmt="e4m3"):
    dtype, down = {"e4m3": (ml_dtypes.float8_e4m3fn, 7), "e5m2": (ml_dtypes.float8_e5m2, 14)}[fmt]
    v = np.moveaxis(np.asarray(x, np.float32).astype(ml_dtypes.bfloat16).astype(np.float64), axis, -1)
    blocks = v.reshape(v.shape[:-1] + (-1, 32))
    amax = np.abs(blocks).max(-1, keepdims=True)
    byte = np.maximum(np.where(amax > 0, np.frexp(amax)[1] - 1 + 127, 0) - down, 1)
    scale = np.exp2(byte - 127.0)
    codes = (blocks / scale).astype(np.float32).astype(dtype).astype(np.float64)
    return np.moveaxis((codes * scale).reshape(v.shape), -1, axis)


WIDE = False


def mx_kscale(k):
    if not WIDE:
        return np.ones(k)
    levels = np.array([10, -10, 5, -5, 0])
    if k % 512:
        return np.exp2(np.random.permutation(np.resize(levels, k // 32))).repeat(32)
    a = np.empty((k // 512, 16))
    for p in range(k // 512):
        a[p, :8] = np.random.permutation(np.resize(levels, 8))
        for g in range(8):
            far = levels[np.abs(levels - a[p, g]) >= 10]
            a[p, g + 8] = far[np.random.randint(len(far))]
    return np.exp2(a.ravel()).repeat(32)


def f64(x):
    return np.asarray(x).astype(np.float64)


def striped(idx):
    return np.tile(idx.reshape(-1, 16).T, (8, 1)).astype(np.uint16)


def unstriped(offs):
    return offs[:16].T.reshape(-1).astype(np.int64)


def striped8(idx):
    return np.concatenate([x.reshape(-1, 16).T for x in idx]).astype(np.uint16)


def runs(offs, k):
    lists = np.stack([offs[16 * r : 16 * r + 16].T.reshape(-1) for r in range(8)]).astype(np.int64)
    return lists[np.arange(k) % 512 // 64]


def pack_weight(w):
    k, n = w.shape
    w = f64(np.asarray(w, np.float32).astype(ml_dtypes.bfloat16)).reshape(k // 32, 32, n)
    amax = np.abs(w).max(1)
    byte = np.clip(np.where(amax > 0, np.frexp(amax)[1] - 1 + 127 - 7, 1), 1, 254)
    scaled = (w * np.exp2(127.0 - byte)[:, None, :]).reshape(k, n).astype(np.float32)
    words = np.ascontiguousarray(scaled.reshape(k // 512, 128, 4, n).transpose(0, 1, 3, 2)).astype(ml_dtypes.float8_e4m3fn).view(np.uint8)
    return words, np.ascontiguousarray(byte.astype(np.uint8).reshape(k // 512, 16, n))


def unpack_weight(words, scales):
    g, p, n, _ = words.shape
    vals = np.ascontiguousarray(words).view(ml_dtypes.float8_e4m3fn).astype(np.float64) * np.repeat(np.exp2(scales.astype(np.float64) - 127.0), 8, axis=1)[..., None]
    return vals.transpose(0, 1, 3, 2).reshape(g * 512, n)


E2M1 = np.array([0.0, 0.5, 1.0, 1.5, 2.0, 3.0, 4.0, 6.0, -0.0, -0.5, -1.0, -1.5, -2.0, -3.0, -4.0, -6.0])


def pack_fp4(w):
    k, n = w.shape
    w = f64(np.asarray(w, np.float32).astype(ml_dtypes.bfloat16)).reshape(k // 32, 32, n)
    amax = np.abs(w).max(1)
    mant, ex = np.frexp(amax / 6.0)
    byte = np.clip(np.where(amax > 0, np.where(mant > 0.5, ex, ex - 1) + 127, 1), 1, 254)
    scaled = (w * np.exp2(127.0 - byte)[:, None, :]).reshape(k, n).astype(np.float32)
    c = np.ascontiguousarray(scaled.reshape(k // 512, 128, 4, n).transpose(0, 1, 3, 2)).astype(ml_dtypes.float4_e2m1fn).view(np.uint8) & 0xF
    words = (c[..., 0::2] | (c[..., 1::2] << 4)).reshape(k // 512, 128, 2 * n)
    return np.ascontiguousarray(words), np.ascontiguousarray(byte.astype(np.uint8).reshape(k // 512, 16, n))


def unpack_fp4(words, scales):
    g, _, n = scales.shape
    words = np.ascontiguousarray(words).reshape(g, 128, n, 2)
    nib = np.empty((g, 128, n, 4), np.uint8)
    nib[..., 0::2] = words & 0xF
    nib[..., 1::2] = words >> 4
    vals = E2M1[nib] * np.repeat(np.exp2(scales.astype(np.float64) - 127.0), 8, axis=1)[..., None]
    return vals.transpose(0, 1, 3, 2).reshape(g * 512, n)


def planes(y):
    n, m = y.shape
    v = y.astype(np.float32).astype(ml_dtypes.bfloat16).astype(np.float64).reshape(n // 32, 32, m)
    top = np.abs(v).max(1)
    byte = np.clip(np.where(top > 0, np.frexp(top)[1] - 1 + 127 - 7, 1), 1, 254)
    codes = (v * np.exp2(127.0 - byte)[:, None, :]).reshape(n, m).astype(np.float32).astype(ml_dtypes.float8_e4m3fn).view(np.uint8)
    words = codes.reshape(n // 512, 128, 4, m).transpose(0, 1, 3, 2)
    return np.ascontiguousarray(words), np.ascontiguousarray(byte.astype(np.uint8).reshape(n // 512, 16, m))


K, T, S, N, G, H = 512, 2048, 512, 512, 2048, 512


def setup_inputs():
    n = np.random.standard_normal
    s = mx_kscale(K)[:, None]
    u = mx_kscale(S)
    packed_xT = pack_weight(n((K, T)) * s)
    packed_dT = pack_weight(n((K, G)) / s)
    packed_w1 = pack_fp4(n((H, N)) / np.sqrt(H) / u[:, None])
    return {
        "x_words": packed_xT[0],
        "x_scales": packed_xT[1],
        "d_words": packed_dT[0],
        "d_scales": packed_dT[1],
        "gn": (np.random.uniform(0.5, 1.5, (H, 1)) * u[:, None]).astype(np.float32),
        "w1_words": packed_w1[0],
        "w1_scales": packed_w1[1],
        "offs": striped(np.random.permutation(T)[:S]),
        "k1": striped8(np.random.randint(0, G, (8, H))),
        "two": striped(np.random.permutation(T)[:S]),
        "n1": striped8(np.stack([np.random.permutation(S) for _ in range(8)])),
        "n2": striped8(np.stack([np.random.permutation(S) for _ in range(8)])),
        "n3": striped(np.random.randint(0, S, G)),
    }


def reference(x_words, x_scales, d_words, d_scales, gn, w1_words, w1_scales, offs, k1, two, n1, n2, n3):
    d_k1 = unpack_weight(d_words, d_scales)[np.arange(K)[:, None], runs(k1, K)]
    xq = unpack_weight(x_words, x_scales)[:, unstriped(offs)]
    a = 0.0625 * (d_k1.T @ xq)
    x_two = unpack_weight(x_words, x_scales)[:, unstriped(two)]
    b = 0.0625 * (d_k1.T @ x_two)
    z = f64(gn) * (a * (np.tanh(b[np.arange(H)[:, None], runs(n1, H)] - (b[np.arange(H)[:, None], runs(n2, H)]))))
    h = unpack_fp4(w1_words, w1_scales).T @ mxq(z, 0, "e4m3")
    mb = h[:, unstriped(n3)]
    mx = mb.reshape(N, S, 4).max(axis=2)
    mn = mb.reshape(N, S, 4).min(axis=2)
    out_0 = mx - (0.5 * mn)
    return (out_0,) + planes(out_0)

@@ -1,0 +1,260 @@
+from contextlib import ExitStack
+
+import concourse.mybir as mybir
+
+K, T, S, N, G, H = 512, 2048, 512, 512, 2048, 512
+FLOPS = 2 * K * H * S * 2 + 2 * H * N * S
+
+F32 = mybir.dt.float32
+BF16 = mybir.dt.bfloat16
+I32 = mybir.dt.int32
+U32 = mybir.dt.uint32
+U16 = mybir.dt.uint16
+U8 = mybir.dt.uint8
+FP8X4 = mybir.dt.float8_e4m3fn_x4
+FP4X4 = mybir.dt.float4_e2m1fn_x4
+ALU = mybir.AluOpType
+ACT = mybir.ActivationFunctionType
+
+P = 128
+PACK = 4
+LANE = 16
+QUAD = 32
+SHIFT = LANE - 2
+SCORE_SCALE = 0.0625
+Z_CHUNKS = (256, 128, 128)
+OUT_CHUNK = 64
+STORE_CHUNKS = 2
+VECTOR_GATHERS = 3
+
+
+def tile_picked_twksjointbgspan_none_po_kernel(
+    tc, x_words, x_scales, d_words, d_scales, gn, w1_words, w1_scales, offs, k1, two, n1, n2, n3, out_0, out_1, out_2
+):
+    nc = tc.nc
+    with ExitStack() as ctx:
+        lists = ctx.enter_context(tc.tile_pool(name="lists", bufs=1))
+        keep = ctx.enter_context(tc.tile_pool(name="keep", bufs=1))
+        ring = ctx.enter_context(tc.tile_pool(name="ring", bufs=3))
+        psum = ctx.enter_context(tc.psum_pool(name="psum", bufs=1))
+
+        def load_list(dram, name):
+            tile = lists.tile(list(dram.shape), U16, name=name)
+            nc.sync.dma_start(tile[:], dram)
+            return tile
+
+        def load_scale_rows(queue, tile, dram, first):
+            for q in range(P // QUAD):
+                lo = QUAD * q + first
+                queue.dma_start(tile[lo : lo + PACK, :].bitcast(I32), dram[0, PACK * q : PACK * (q + 1), :].bitcast(I32))
+
+        def entries(tile, lo, count):
+            return tile[:, lo // LANE : (lo + count) // LANE]
+
+        d_sc = keep.tile([P, G], U8, name="d_sc")
+        x_sc = keep.tile([P, T], U8, name="x_sc")
+        key_sc = keep.tile([P, H], U8, name="key_sc", align_bytes=64)
+        w_sc_raw = keep.tile([P, N], U8, name="w_sc_raw")
+        z_sc = [keep.tile([P, w], U8, name=f"z_sc{c}", align_bytes=64) for c, w in enumerate(Z_CHUNKS)]
+        for tile in (d_sc, x_sc, w_sc_raw, key_sc, *z_sc):
+            nc.vector.memset(tile[:].bitcast(I32), 0)
+
+        d_wd = keep.tile([P, G], U32, name="d_wd")
+        x_wd = keep.tile([P, T], U32, name="x_wd")
+        nc.scalar.dma_start(d_wd[:].bitcast(I32), d_words[0].rearrange("p n t -> p (n t)").bitcast(I32))
+        nc.scalar.dma_start(x_wd[:].bitcast(I32), x_words[0].rearrange("p n t -> p (n t)").bitcast(I32))
+        k1_t = load_list(k1, "k1_t")
+        two_t = load_list(two, "two_t")
+        load_scale_rows(nc.sync, d_sc, d_scales, SHIFT)
+        load_scale_rows(nc.sync, x_sc, x_scales, 0)
+        offs_t = load_list(offs, "offs_t")
+        load_scale_rows(nc.gpsimd, w_sc_raw, w1_scales, 0)
+        gn_t = keep.tile([P, PACK], F32, name="gn_t")
+        nc.gpsimd.dma_start(gn_t[:], gn.rearrange("(p t) o -> p (t o)", t=PACK))
+        w_wd_raw = keep.tile([P, 2 * N], U8, name="w_wd_raw")
+        nc.sync.dma_start(w_wd_raw[:].bitcast(I32), w1_words[0].bitcast(I32))
+        n1_t = load_list(n1, "n1_t")
+        n2_t = load_list(n2, "n2_t")
+        n3_t = load_list(n3, "n3_t")
+
+        key_sc_got = keep.tile([P, H], U8, name="key_sc_got")
+        nc.vector.tensor_copy(key_sc_got[:], d_sc[:].indirect(k1_t[:]))
+        key_sc_dealt = keep.tile([P, H], U8, name="key_sc_dealt")
+        nc.vector.tensor_copy(
+            key_sc_dealt[:].rearrange("p (t m) -> p t m", t=PACK), key_sc_got[:].rearrange("p (m t) -> p t m", t=PACK)
+        )
+        span = P - QUAD + PACK
+        nc.scalar.dma_start(key_sc[0:span, :].bitcast(I32), key_sc_dealt[SHIFT : SHIFT + span, :].bitcast(I32))
+        key_wd_got = keep.tile([P, H], U32, name="key_wd_got")
+        nc.vector.tensor_copy(key_wd_got[:], d_wd[:].indirect(k1_t[:]))
+        key_wd = keep.tile([P, H], U32, name="key_wd", align_bytes=64)
+        nc.vector.tensor_copy(
+            key_wd[:].rearrange("p (t m) -> p t m", t=PACK), key_wd_got[:].rearrange("p (m t) -> p t m", t=PACK)
+        )
+
+        def scores(list_t, name):
+            tok_sc = keep.tile([P, S], U8, name=name + "_sc", align_bytes=64)
+            nc.vector.tensor_copy(tok_sc[:], x_sc[:].indirect(list_t[:]))
+            tok_wd = keep.tile([P, S], U32, name=name + "_wd", align_bytes=64)
+            nc.vector.tensor_copy(tok_wd[:], x_wd[:].indirect(list_t[:]))
+            banks = []
+            for t in range(PACK):
+                bank = psum.tile([P, S], F32, name=f"{name}{t}", tag=f"{name}{t}")
+                cols = slice(t * P, (t + 1) * P)
+                nc.tensor.matmul_mx(
+                    out=bank[:],
+                    lhsT=key_wd[:, cols].bitcast(FP8X4),
+                    lhsT_scale=key_sc[:, cols],
+                    rhs=tok_wd[:].bitcast(FP8X4),
+                    rhs_scale=tok_sc[:],
+                    start=True,
+                    stop=True,
+                )
+                banks.append(bank)
+            return banks
+
+        b_banks = scores(two_t, "b")
+
+        w_wd = keep.tile([P, 2 * N], U8, name="w_wd", align_bytes=64)
+        nc.scalar.copy(
+            w_wd[:].bitcast(U16).rearrange("p (t m) -> p t m", t=PACK),
+            w_wd_raw[:].bitcast(U16).rearrange("p (m t) -> p t m", t=PACK),
+        )
+        w_sc = keep.tile([P, N], U8, name="w_sc", align_bytes=64)
+        nc.gpsimd.tensor_copy(
+            w_sc[:].rearrange("p (t m) -> p t m", t=PACK), w_sc_raw[:].rearrange("p (m t) -> p t m", t=PACK)
+        )
+        gain = keep.tile([P, PACK], F32, name="gain")
+        nc.gpsimd.tensor_scalar(gain[:], gn_t[:], SCORE_SCALE, 0.0, ALU.mult, ALU.add)
+
+        starts = [sum(Z_CHUNKS[:c]) for c in range(len(Z_CHUNKS))]
+        units = [(c, t) for c in range(len(Z_CHUNKS)) for t in range(PACK)]
+        b_rows = [keep.tile([P, S], F32, name=f"b_row{t}") for t in range(PACK)]
+        h_rows = [keep.tile([P, S], F32, name=f"h_row{t}") for t in range(PACK)]
+        first = [keep.tile([P, Z_CHUNKS[c]], F32, name=f"first{c}{t}") for c, t in units]
+        diff = [keep.tile([P, Z_CHUNKS[c]], F32, name=f"diff{c}{t}") for c, t in units]
+        gate = [keep.tile([P, Z_CHUNKS[c]], F32, name=f"gate{c}{t}") for c, t in units]
+        z_planes = [keep.tile([P, PACK, w], BF16, name=f"z_planes{c}") for c, w in enumerate(Z_CHUNKS)]
+        z_grouped = [keep.tile([P, w, PACK], BF16, name=f"z_grouped{c}", align_bytes=64) for c, w in enumerate(Z_CHUNKS)]
+        z_wd = [keep.tile([P, w], U32, name=f"z_wd{c}", align_bytes=64) for c, w in enumerate(Z_CHUNKS)]
+
+        def fetch_first(u):
+            c, t = units[u]
+            nc.scalar.activation(first[u][:], b_rows[t][:].indirect(entries(n1_t, starts[c], Z_CHUNKS[c])), ACT.Copy)
+
+        def fetch_second(u):
+            c, t = units[u]
+            nc.vector.tensor_tensor(
+                diff[u][:], b_rows[t][:].indirect(entries(n2_t, starts[c], Z_CHUNKS[c])), first[u][:], ALU.subtract
+            )
+
+        def squash(u):
+            nc.scalar.activation(gate[u][:], diff[u][:], ACT.Tanh, scale=-SCORE_SCALE)
+
+        def apply_gate(u):
+            c, t = units[u]
+            cols = slice(starts[c], starts[c] + Z_CHUNKS[c])
+            nc.vector.scalar_tensor_tensor(
+                z_planes[c][:, t, :], a_banks[t][:, cols], gain[:, t : t + 1], gate[u][:], ALU.mult, ALU.mult
+            )
+
+        def group_z(c):
+            nc.vector.tensor_copy(
+                z_grouped[c][:].rearrange("p (c i) t -> p c t i", i=PACK),
+                z_planes[c][:].rearrange("p t (c i) -> p c t i", i=PACK),
+            )
+
+        def layer(c):
+            width = Z_CHUNKS[c]
+            nc.vector.quantize_mx(
+                out=z_wd[c][:].bitcast(FP8X4), scales=z_sc[c][:], in_=z_grouped[c][:].rearrange("p w t -> p (w t)")
+            )
+            per_bank = S // width
+            for t in range(PACK):
+                if t % per_bank == 0:
+                    bank_no = (PACK * starts[c] + t * width) // S
+                    h_bank = psum.tile([P, S], F32, name=f"h{bank_no}", tag=f"b{bank_no}")
+                slot = slice((t % per_bank) * width, (t % per_bank + 1) * width)
+                nc.tensor.matmul_mx(
+                    out=h_bank[:, slot],
+                    lhsT=w_wd[:, 2 * t * P : 2 * (t + 1) * P].bitcast(FP4X4),
+                    lhsT_scale=w_sc[:, t * P : (t + 1) * P],
+                    rhs=z_wd[c][:].bitcast(FP8X4),
+                    rhs_scale=z_sc[c][:],
+                    start=True,
+                    stop=True,
+                )
+                if t % per_bank == per_bank - 1:
+                    for s in range(per_bank):
+                        row = h_rows[t + 1 - per_bank + s]
+                        nc.scalar.copy(row[:, starts[c] : starts[c] + width], h_bank[:, s * width : (s + 1) * width])
+
+        for t in range(PACK):
+            nc.scalar.copy(b_rows[t][:], b_banks[t][:])
+            fetch_first(t)
+        a_banks = scores(offs_t, "a")
+        for step in range(len(units) + 4):
+            if step < len(units):
+                fetch_second(step)
+            if step + PACK < len(units):
+                fetch_first(step + PACK)
+            if 1 <= step <= len(units):
+                squash(step - 1)
+            if 2 <= step <= len(units) + 1:
+                apply_gate(step - 2)
+            if step >= PACK + 2 and (step - 2) % PACK == 0:
+                group_z((step - 2) // PACK - 1)
+            if step >= PACK + 3 and (step - 3) % PACK == 0:
+                layer((step - 3) // PACK - 1)
+
+        y_wd = keep.tile([P, S], U32, name="y_wd", align_bytes=64)
+        y_sc = keep.tile([P, S], U8, name="y_sc", align_bytes=64)
+        out_rows = out_0.rearrange("(p t) j -> p t j", t=PACK)
+        out_wd = out_1[0].rearrange("p n t -> p (n t)").bitcast(I32)
+        picks = PACK * OUT_CHUNK
+        chunks = S // OUT_CHUNK
+        groups = PACK * OUT_CHUNK
+        for c in range(chunks + 1):
+            if c < chunks:
+                members = ring.tile([P, PACK, picks], F32, name="members")
+                for t in range(PACK):
+                    window = h_rows[t][:].indirect(entries(n3_t, c * picks, picks))
+                    if PACK * c + t < 2 * VECTOR_GATHERS and t % 2 == 1:
+                        nc.vector.tensor_copy(members[:, t, :], window)
+                    else:
+                        nc.scalar.activation(members[:, t, :], window, ACT.Copy)
+                quads = members[:].rearrange("p t (j u v) -> p (t j) u v", u=2, v=2)
+                hi2 = ring.tile([P, groups, 2], F32, name="hi2")
+                lo2 = ring.tile([P, groups, 2], F32, name="lo2")
+                nc.vector.tensor_tensor(lo2[:], quads[:, :, 0, :], quads[:, :, 1, :], ALU.min)
+                nc.vector.tensor_tensor(hi2[:], quads[:, :, 0, :], quads[:, :, 1, :], ALU.max)
+            if c >= 1:
+                cols = slice((c - 1) * OUT_CHUNK, c * OUT_CHUNK)
+                y = keep.tile([P, PACK, OUT_CHUNK], F32, name=f"y{c - 1}")
+                nc.vector.scalar_tensor_tensor(
+                    y[:].rearrange("p t j -> p (t j)"), smallest[:], -0.5, largest[:], ALU.mult, ALU.add
+                )
+                nc.sync.dma_start(out_rows[:, :, cols], y[:])
+            if c < chunks:
+                smallest = ring.tile([P, groups], F32, name="smallest")
+                nc.vector.tensor_tensor(smallest[:], lo2[:, :, 0], lo2[:, :, 1], ALU.min)
+            if c >= 1:
+                y_grouped = ring.tile([P, OUT_CHUNK, PACK], BF16, name="y_grouped", align_bytes=64)
+                nc.vector.tensor_copy(
+                    y_grouped[:].rearrange("p (c i) t -> p c t i", i=PACK), y[:].rearrange("p t (c i) -> p c t i", i=PACK)
+                )
+            if c < chunks:
+                largest = ring.tile([P, groups], F32, name="largest")
+                nc.vector.tensor_tensor(largest[:], hi2[:, :, 0], hi2[:, :, 1], ALU.max)
+            if c >= 1:
+                nc.vector.quantize_mx(
+                    out=y_wd[:, cols].bitcast(FP8X4), scales=y_sc[:, cols], in_=y_grouped[:].rearrange("p w t -> p (w t)")
+                )
+                if c % STORE_CHUNKS == 0:
+                    done = slice((c - STORE_CHUNKS) * OUT_CHUNK, c * OUT_CHUNK)
+                    nc.sync.dma_start(out_wd[:, done], y_wd[:, done].bitcast(I32))
+        for q in range(P // QUAD):
+            queue = nc.sync if q % 2 == 0 else nc.scalar
+            queue.dma_start(
+                out_2[0, PACK * q : PACK * (q + 1), :].bitcast(I32), y_sc[QUAD * q : QUAD * q + PACK, :].bitcast(I32)
+            )

@@ -20,12 +20,11 @@ P = 128
 PACK = 4
 LANE = 16
 QUAD = 32
-SHIFT = LANE - 2
+BLOCK = 8
+SPARE = 32
 SCORE_SCALE = 0.0625
 Z_CHUNKS = (256, 128, 128)
-OUT_CHUNK = 64
-STORE_CHUNKS = 2
-VECTOR_GATHERS = 3
+OUT_CHUNKS = (64, 128, 128, 128, 64)
 
 
 def tile_picked_twksjointbgspan_none_po_kernel(
@@ -43,48 +42,56 @@ def tile_picked_twksjointbgspan_none_po_kernel(
             nc.sync.dma_start(tile[:], dram)
             return tile
 
-        def load_scale_rows(queue, tile, dram, first):
+        def load_scale_rows(queue, tile, dram):
             for q in range(P // QUAD):
-                lo = QUAD * q + first
+                lo = QUAD * q
                 queue.dma_start(tile[lo : lo + PACK, :].bitcast(I32), dram[0, PACK * q : PACK * (q + 1), :].bitcast(I32))
 
         def entries(tile, lo, count):
             return tile[:, lo // LANE : (lo + count) // LANE]
 
-        d_sc = keep.tile([P, G], U8, name="d_sc")
         x_sc = keep.tile([P, T], U8, name="x_sc")
-        key_sc = keep.tile([P, H], U8, name="key_sc", align_bytes=64)
         w_sc_raw = keep.tile([P, N], U8, name="w_sc_raw")
+        for tile in (x_sc, w_sc_raw):
+            nc.gpsimd.memset(tile[:].bitcast(I32), 0)
         z_sc = [keep.tile([P, w], U8, name=f"z_sc{c}", align_bytes=64) for c, w in enumerate(Z_CHUNKS)]
-        for tile in (d_sc, x_sc, w_sc_raw, key_sc, *z_sc):
+        for tile in z_sc:
             nc.vector.memset(tile[:].bitcast(I32), 0)
+        h_rows = [keep.tile([P, S + SPARE], F32, name=f"h_row{t}") for t in range(PACK)]
+        for tile in h_rows:
+            nc.vector.memset(tile[:, S:], 0.0)
 
+        d_sc = keep.tile([P, G], U8, name="d_sc")
         d_wd = keep.tile([P, G], U32, name="d_wd")
         x_wd = keep.tile([P, T], U32, name="x_wd")
-        nc.scalar.dma_start(d_wd[:].bitcast(I32), d_words[0].rearrange("p n t -> p (n t)").bitcast(I32))
-        nc.scalar.dma_start(x_wd[:].bitcast(I32), x_words[0].rearrange("p n t -> p (n t)").bitcast(I32))
         k1_t = load_list(k1, "k1_t")
+        nc.sync.dma_start(
+            d_sc[:].bitcast(I32), d_scales[0].bitcast(I32).unsqueeze(1).broadcast_to([K // QUAD, BLOCK, G // PACK])
+        )
+        nc.sync.dma_start(d_wd[:].bitcast(I32), d_words[0].rearrange("p n t -> p (n t)").bitcast(I32))
         two_t = load_list(two, "two_t")
-        load_scale_rows(nc.sync, d_sc, d_scales, SHIFT)
-        load_scale_rows(nc.sync, x_sc, x_scales, 0)
+        load_scale_rows(nc.sync, x_sc, x_scales)
         offs_t = load_list(offs, "offs_t")
-        load_scale_rows(nc.gpsimd, w_sc_raw, w1_scales, 0)
+        nc.sync.dma_start(x_wd[:].bitcast(I32), x_words[0].rearrange("p n t -> p (n t)").bitcast(I32))
         gn_t = keep.tile([P, PACK], F32, name="gn_t")
         nc.gpsimd.dma_start(gn_t[:], gn.rearrange("(p t) o -> p (t o)", t=PACK))
-        w_wd_raw = keep.tile([P, 2 * N], U8, name="w_wd_raw")
-        nc.sync.dma_start(w_wd_raw[:].bitcast(I32), w1_words[0].bitcast(I32))
+        load_scale_rows(nc.gpsimd, w_sc_raw, w1_scales)
+        gain = keep.tile([P, PACK], F32, name="gain")
+        nc.scalar.activation(gain[:], gn_t[:], ACT.Copy, scale=SCORE_SCALE)
         n1_t = load_list(n1, "n1_t")
         n2_t = load_list(n2, "n2_t")
+        w_wd_raw = keep.tile([P, 2 * N], U8, name="w_wd_raw")
+        nc.sync.dma_start(w_wd_raw[:].bitcast(I32), w1_words[0].bitcast(I32))
         n3_t = load_list(n3, "n3_t")
 
         key_sc_got = keep.tile([P, H], U8, name="key_sc_got")
         nc.vector.tensor_copy(key_sc_got[:], d_sc[:].indirect(k1_t[:]))
-        key_sc_dealt = keep.tile([P, H], U8, name="key_sc_dealt")
+        key_sc = keep.tile([P, H], U8, name="key_sc", align_bytes=64)
         nc.vector.tensor_copy(
-            key_sc_dealt[:].rearrange("p (t m) -> p t m", t=PACK), key_sc_got[:].rearrange("p (m t) -> p t m", t=PACK)
+            key_sc[:].rearrange("p (t m) -> p t m", t=PACK), key_sc_got[:].rearrange("p (m t) -> p t m", t=PACK)
         )
-        span = P - QUAD + PACK
-        nc.scalar.dma_start(key_sc[0:span, :].bitcast(I32), key_sc_dealt[SHIFT : SHIFT + span, :].bitcast(I32))
+        for r in range(1, PACK):
+            nc.scalar.dma_start(key_sc[r:P:QUAD, :].bitcast(I32), key_sc[BLOCK * r : P : QUAD, :].bitcast(I32))
         key_wd_got = keep.tile([P, H], U32, name="key_wd_got")
         nc.vector.tensor_copy(key_wd_got[:], d_wd[:].indirect(k1_t[:]))
         key_wd = keep.tile([P, H], U32, name="key_wd", align_bytes=64)
@@ -124,13 +131,10 @@ def tile_picked_twksjointbgspan_none_po_kernel(
         nc.gpsimd.tensor_copy(
             w_sc[:].rearrange("p (t m) -> p t m", t=PACK), w_sc_raw[:].rearrange("p (m t) -> p t m", t=PACK)
         )
-        gain = keep.tile([P, PACK], F32, name="gain")
-        nc.gpsimd.tensor_scalar(gain[:], gn_t[:], SCORE_SCALE, 0.0, ALU.mult, ALU.add)
 
         starts = [sum(Z_CHUNKS[:c]) for c in range(len(Z_CHUNKS))]
         units = [(c, t) for c in range(len(Z_CHUNKS)) for t in range(PACK)]
         b_rows = [keep.tile([P, S], F32, name=f"b_row{t}") for t in range(PACK)]
-        h_rows = [keep.tile([P, S], F32, name=f"h_row{t}") for t in range(PACK)]
         first = [keep.tile([P, Z_CHUNKS[c]], F32, name=f"first{c}{t}") for c, t in units]
         diff = [keep.tile([P, Z_CHUNKS[c]], F32, name=f"diff{c}{t}") for c, t in units]
         gate = [keep.tile([P, Z_CHUNKS[c]], F32, name=f"gate{c}{t}") for c, t in units]
@@ -169,11 +173,12 @@ def tile_picked_twksjointbgspan_none_po_kernel(
             nc.vector.quantize_mx(
                 out=z_wd[c][:].bitcast(FP8X4), scales=z_sc[c][:], in_=z_grouped[c][:].rearrange("p w t -> p (w t)")
             )
-            per_bank = S // width
+            last = c == len(Z_CHUNKS) - 1
+            per_bank = 1 if last else S // width
             for t in range(PACK):
                 if t % per_bank == 0:
-                    bank_no = (PACK * starts[c] + t * width) // S
-                    h_bank = psum.tile([P, S], F32, name=f"h{bank_no}", tag=f"b{bank_no}")
+                    tag = f"a{t}" if last else f"b{(PACK * starts[c] + t * width) // S}"
+                    h_bank = psum.tile([P, S], F32, name=f"h{c}{t}", tag=tag)
                 slot = slice((t % per_bank) * width, (t % per_bank + 1) * width)
                 nc.tensor.matmul_mx(
                     out=h_bank[:, slot],
@@ -186,8 +191,11 @@ def tile_picked_twksjointbgspan_none_po_kernel(
                 )
                 if t % per_bank == per_bank - 1:
                     for s in range(per_bank):
-                        row = h_rows[t + 1 - per_bank + s]
-                        nc.scalar.copy(row[:, starts[c] : starts[c] + width], h_bank[:, s * width : (s + 1) * width])
+                        row = h_rows[t + 1 - per_bank + s][:, starts[c] : starts[c] + width]
+                        if last and t % 2 == 1:
+                            nc.vector.tensor_copy(row, h_bank[:, s * width : (s + 1) * width])
+                        else:
+                            nc.scalar.copy(row, h_bank[:, s * width : (s + 1) * width])
 
         for t in range(PACK):
             nc.scalar.copy(b_rows[t][:], b_banks[t][:])
@@ -211,48 +219,66 @@ def tile_picked_twksjointbgspan_none_po_kernel(
         y_sc = keep.tile([P, S], U8, name="y_sc", align_bytes=64)
         out_rows = out_0.rearrange("(p t) j -> p t j", t=PACK)
         out_wd = out_1[0].rearrange("p n t -> p (n t)").bitcast(I32)
-        picks = PACK * OUT_CHUNK
-        chunks = S // OUT_CHUNK
-        groups = PACK * OUT_CHUNK
-        for c in range(chunks + 1):
-            if c < chunks:
-                members = ring.tile([P, PACK, picks], F32, name="members")
-                for t in range(PACK):
-                    window = h_rows[t][:].indirect(entries(n3_t, c * picks, picks))
-                    if PACK * c + t < 2 * VECTOR_GATHERS and t % 2 == 1:
-                        nc.vector.tensor_copy(members[:, t, :], window)
-                    else:
-                        nc.scalar.activation(members[:, t, :], window, ACT.Copy)
-                quads = members[:].rearrange("p t (j u v) -> p (t j) u v", u=2, v=2)
-                hi2 = ring.tile([P, groups, 2], F32, name="hi2")
-                lo2 = ring.tile([P, groups, 2], F32, name="lo2")
-                nc.vector.tensor_tensor(lo2[:], quads[:, :, 0, :], quads[:, :, 1, :], ALU.min)
-                nc.vector.tensor_tensor(hi2[:], quads[:, :, 0, :], quads[:, :, 1, :], ALU.max)
-            if c >= 1:
-                cols = slice((c - 1) * OUT_CHUNK, c * OUT_CHUNK)
-                y = keep.tile([P, PACK, OUT_CHUNK], F32, name=f"y{c - 1}")
-                nc.vector.scalar_tensor_tensor(
-                    y[:].rearrange("p t j -> p (t j)"), smallest[:], -0.5, largest[:], ALU.mult, ALU.add
-                )
-                nc.sync.dma_start(out_rows[:, :, cols], y[:])
-            if c < chunks:
-                smallest = ring.tile([P, groups], F32, name="smallest")
-                nc.vector.tensor_tensor(smallest[:], lo2[:, :, 0], lo2[:, :, 1], ALU.min)
-            if c >= 1:
-                y_grouped = ring.tile([P, OUT_CHUNK, PACK], BF16, name="y_grouped", align_bytes=64)
-                nc.vector.tensor_copy(
-                    y_grouped[:].rearrange("p (c i) t -> p c t i", i=PACK), y[:].rearrange("p t (c i) -> p c t i", i=PACK)
-                )
-            if c < chunks:
-                largest = ring.tile([P, groups], F32, name="largest")
-                nc.vector.tensor_tensor(largest[:], hi2[:, :, 0], hi2[:, :, 1], ALU.max)
-            if c >= 1:
-                nc.vector.quantize_mx(
-                    out=y_wd[:, cols].bitcast(FP8X4), scales=y_sc[:, cols], in_=y_grouped[:].rearrange("p w t -> p (w t)")
-                )
-                if c % STORE_CHUNKS == 0:
-                    done = slice((c - STORE_CHUNKS) * OUT_CHUNK, c * OUT_CHUNK)
-                    nc.sync.dma_start(out_wd[:, done], y_wd[:, done].bitcast(I32))
+        out_starts = [sum(OUT_CHUNKS[:c]) for c in range(len(OUT_CHUNKS))]
+        halves = [(c, half) for c in range(len(OUT_CHUNKS)) for half in range(2)]
+        ys = [keep.tile([P, PACK, w], F32, name=f"y{c}") for c, w in enumerate(OUT_CHUNKS)]
+        y_grouped = [keep.tile([P, w, PACK], BF16, name=f"y_grouped{c}", align_bytes=64) for c, w in enumerate(OUT_CHUNKS)]
+
+        def fetch_and_pair(u):
+            c, half = halves[u]
+            picks = PACK * OUT_CHUNKS[c]
+            members = ring.tile([P, 2, picks], F32, name="members")
+            for s in range(2):
+                window = h_rows[2 * half + s][:].indirect(entries(n3_t, PACK * out_starts[c], picks))
+                if c == 0 and s == 1:
+                    nc.vector.tensor_copy(members[:, s, :], window)
+                else:
+                    nc.scalar.activation(members[:, s, :], window, ACT.Copy)
+            quads = members[:].rearrange("p t (j u v) -> p (t j) u v", u=2, v=2)
+            hi2 = ring.tile([P, 2 * OUT_CHUNKS[c], 2], F32, name="hi2")
+            lo2 = ring.tile([P, 2 * OUT_CHUNKS[c], 2], F32, name="lo2")
+            nc.vector.tensor_tensor(lo2[:], quads[:, :, 0, :], quads[:, :, 1, :], ALU.min)
+            nc.vector.tensor_tensor(hi2[:], quads[:, :, 0, :], quads[:, :, 1, :], ALU.max)
+            return hi2, lo2
+
+        def finish(pairs, op, name):
+            tile = ring.tile([P, pairs.shape[1]], F32, name=name)
+            nc.vector.tensor_tensor(tile[:], pairs[:, :, 0], pairs[:, :, 1], op)
+            return tile
+
+        def combine(u, top, low):
+            c, half = halves[u]
+            nc.vector.scalar_tensor_tensor(
+                ys[c][:, 2 * half : 2 * half + 2, :].rearrange("p t j -> p (t j)"), low[:], -0.5, top[:], ALU.mult, ALU.add
+            )
+            if half == 1:
+                nc.sync.dma_start(out_rows[:, :, out_starts[c] : out_starts[c] + OUT_CHUNKS[c]], ys[c][:])
+
+        def group_y(c):
+            nc.vector.tensor_copy(
+                y_grouped[c][:].rearrange("p (c i) t -> p c t i", i=PACK), ys[c][:].rearrange("p t (c i) -> p c t i", i=PACK)
+            )
+
+        def quantise_y(c):
+            cols = slice(out_starts[c], out_starts[c] + OUT_CHUNKS[c])
+            nc.vector.quantize_mx(
+                out=y_wd[:, cols].bitcast(FP8X4), scales=y_sc[:, cols], in_=y_grouped[c][:].rearrange("p w t -> p (w t)")
+            )
+            nc.sync.dma_start(out_wd[:, cols], y_wd[:, cols].bitcast(I32))
+
+        for u in range(len(halves) + 1):
+            if u < len(halves):
+                hi2, lo2 = fetch_and_pair(u)
+            if u >= 1:
+                combine(u - 1, top, low)
+            if u < len(halves):
+                low = finish(lo2, ALU.min, "low")
+            if u >= 2 and u % 2 == 0:
+                group_y(u // 2 - 1)
+            if u < len(halves):
+                top = finish(hi2, ALU.max, "top")
+            if u >= 2 and u % 2 == 0:
+                quantise_y(u // 2 - 1)
         for q in range(P // QUAD):
             queue = nc.sync if q % 2 == 0 else nc.scalar
             queue.dma_start(

@@ -23,8 +23,10 @@ QUAD = 32
 BLOCK = 8
 SPARE = 32
 SCORE_SCALE = 0.0625
-Z_CHUNKS = (256, 128, 128)
+Z_CHUNKS = (256, 256)
 OUT_CHUNKS = (64, 128, 128, 128, 64)
+SCALAR_GROUPS = (3,)
+VECTOR_FETCHES = ((0, 1), (0, 3), (1, 1))
 
 
 def tile_picked_twksjointbgspan_none_po_kernel(
@@ -52,8 +54,8 @@ def tile_picked_twksjointbgspan_none_po_kernel(
 
         x_sc = keep.tile([P, T], U8, name="x_sc")
         w_sc_raw = keep.tile([P, N], U8, name="w_sc_raw")
-        for tile in (x_sc, w_sc_raw):
-            nc.gpsimd.memset(tile[:].bitcast(I32), 0)
+        nc.vector.memset(x_sc[:].bitcast(I32), 0)
+        nc.gpsimd.memset(w_sc_raw[:].bitcast(I32), 0)
         z_sc = [keep.tile([P, w], U8, name=f"z_sc{c}", align_bytes=64) for c, w in enumerate(Z_CHUNKS)]
         for tile in z_sc:
             nc.vector.memset(tile[:].bitcast(I32), 0)
@@ -65,24 +67,24 @@ def tile_picked_twksjointbgspan_none_po_kernel(
         d_wd = keep.tile([P, G], U32, name="d_wd")
         x_wd = keep.tile([P, T], U32, name="x_wd")
         k1_t = load_list(k1, "k1_t")
+        two_t = load_list(two, "two_t")
         nc.sync.dma_start(
             d_sc[:].bitcast(I32), d_scales[0].bitcast(I32).unsqueeze(1).broadcast_to([K // QUAD, BLOCK, G // PACK])
         )
-        nc.sync.dma_start(d_wd[:].bitcast(I32), d_words[0].rearrange("p n t -> p (n t)").bitcast(I32))
-        two_t = load_list(two, "two_t")
-        load_scale_rows(nc.sync, x_sc, x_scales)
-        offs_t = load_list(offs, "offs_t")
         nc.sync.dma_start(x_wd[:].bitcast(I32), x_words[0].rearrange("p n t -> p (n t)").bitcast(I32))
+        nc.sync.dma_start(d_wd[:].bitcast(I32), d_words[0].rearrange("p n t -> p (n t)").bitcast(I32))
+        load_scale_rows(nc.scalar, x_sc, x_scales)
+        offs_t = load_list(offs, "offs_t")
+        n1_t = load_list(n1, "n1_t")
+        n2_t = load_list(n2, "n2_t")
+        n3_t = load_list(n3, "n3_t")
         gn_t = keep.tile([P, PACK], F32, name="gn_t")
         nc.gpsimd.dma_start(gn_t[:], gn.rearrange("(p t) o -> p (t o)", t=PACK))
+        w_wd_raw = keep.tile([P, 2 * N], U8, name="w_wd_raw")
+        nc.gpsimd.dma_start(w_wd_raw[:].bitcast(I32), w1_words[0].bitcast(I32))
         load_scale_rows(nc.gpsimd, w_sc_raw, w1_scales)
         gain = keep.tile([P, PACK], F32, name="gain")
         nc.scalar.activation(gain[:], gn_t[:], ACT.Copy, scale=SCORE_SCALE)
-        n1_t = load_list(n1, "n1_t")
-        n2_t = load_list(n2, "n2_t")
-        w_wd_raw = keep.tile([P, 2 * N], U8, name="w_wd_raw")
-        nc.sync.dma_start(w_wd_raw[:].bitcast(I32), w1_words[0].bitcast(I32))
-        n3_t = load_list(n3, "n3_t")
 
         key_sc_got = keep.tile([P, H], U8, name="key_sc_got")
         nc.vector.tensor_copy(key_sc_got[:], d_sc[:].indirect(k1_t[:]))
@@ -92,18 +94,16 @@ def tile_picked_twksjointbgspan_none_po_kernel(
         )
         for r in range(1, PACK):
             nc.scalar.dma_start(key_sc[r:P:QUAD, :].bitcast(I32), key_sc[BLOCK * r : P : QUAD, :].bitcast(I32))
-        key_wd_got = keep.tile([P, H], U32, name="key_wd_got")
-        nc.vector.tensor_copy(key_wd_got[:], d_wd[:].indirect(k1_t[:]))
-        key_wd = keep.tile([P, H], U32, name="key_wd", align_bytes=64)
-        nc.vector.tensor_copy(
-            key_wd[:].rearrange("p (t m) -> p t m", t=PACK), key_wd_got[:].rearrange("p (m t) -> p t m", t=PACK)
-        )
 
-        def scores(list_t, name):
-            tok_sc = keep.tile([P, S], U8, name=name + "_sc", align_bytes=64)
-            nc.vector.tensor_copy(tok_sc[:], x_sc[:].indirect(list_t[:]))
-            tok_wd = keep.tile([P, S], U32, name=name + "_wd", align_bytes=64)
+        def pick_tokens(list_t, name, tags):
+            tok_wd = keep.tile([P, S], U32, name=name + "_wd", tag=tags[1], align_bytes=64)
             nc.vector.tensor_copy(tok_wd[:], x_wd[:].indirect(list_t[:]))
+            tok_sc = keep.tile([P, S], U8, name=name + "_sc", tag=tags[0], align_bytes=64)
+            nc.vector.tensor_copy(tok_sc[:], x_sc[:].indirect(list_t[:]))
+            return tok_wd, tok_sc
+
+        def scores(tokens, name):
+            tok_wd, tok_sc = tokens
             banks = []
             for t in range(PACK):
                 bank = psum.tile([P, S], F32, name=f"{name}{t}", tag=f"{name}{t}")
@@ -120,7 +120,20 @@ def tile_picked_twksjointbgspan_none_po_kernel(
                 banks.append(bank)
             return banks
 
-        b_banks = scores(two_t, "b")
+        b_tokens = pick_tokens(two_t, "b", ("b_sc", "b_wd"))
+        key_wd = keep.tile([P, H], U32, name="key_wd", align_bytes=64)
+        half = H // 2
+        gots = []
+        for u in range(2):
+            got = keep.tile([P, half], U32, name=f"key_wd_got{u}", tag=f"staged{u}", align_bytes=64)
+            nc.vector.tensor_copy(got[:], d_wd[:].indirect(entries(k1_t, u * half, half)))
+            gots.append(got)
+        for u in range(2):
+            nc.vector.tensor_copy(
+                key_wd[:].rearrange("p (t m) -> p t m", t=PACK)[:, :, u * P // 2 : (u + 1) * P // 2],
+                gots[u][:].rearrange("p (m t) -> p t m", t=PACK),
+            )
+        b_banks = scores(b_tokens, "b")
 
         w_wd = keep.tile([P, 2 * N], U8, name="w_wd", align_bytes=64)
         nc.scalar.copy(
@@ -200,7 +213,7 @@ def tile_picked_twksjointbgspan_none_po_kernel(
         for t in range(PACK):
             nc.scalar.copy(b_rows[t][:], b_banks[t][:])
             fetch_first(t)
-        a_banks = scores(offs_t, "a")
+        a_banks = scores(pick_tokens(offs_t, "a", ("staged0", "staged1")), "a")
         for step in range(len(units) + 4):
             if step < len(units):
                 fetch_second(step)
@@ -224,22 +237,22 @@ def tile_picked_twksjointbgspan_none_po_kernel(
         ys = [keep.tile([P, PACK, w], F32, name=f"y{c}") for c, w in enumerate(OUT_CHUNKS)]
         y_grouped = [keep.tile([P, w, PACK], BF16, name=f"y_grouped{c}", align_bytes=64) for c, w in enumerate(OUT_CHUNKS)]
 
-        def fetch_and_pair(u):
+        def fetch(u):
             c, half = halves[u]
             picks = PACK * OUT_CHUNKS[c]
-            members = ring.tile([P, 2, picks], F32, name="members")
+            members = ring.tile([P, 2, picks], F32, name="members", bufs=4)
             for s in range(2):
                 window = h_rows[2 * half + s][:].indirect(entries(n3_t, PACK * out_starts[c], picks))
-                if c == 0 and s == 1:
+                if (c, 2 * half + s) in VECTOR_FETCHES:
                     nc.vector.tensor_copy(members[:, s, :], window)
                 else:
                     nc.scalar.activation(members[:, s, :], window, ACT.Copy)
-            quads = members[:].rearrange("p t (j u v) -> p (t j) u v", u=2, v=2)
-            hi2 = ring.tile([P, 2 * OUT_CHUNKS[c], 2], F32, name="hi2")
-            lo2 = ring.tile([P, 2 * OUT_CHUNKS[c], 2], F32, name="lo2")
-            nc.vector.tensor_tensor(lo2[:], quads[:, :, 0, :], quads[:, :, 1, :], ALU.min)
-            nc.vector.tensor_tensor(hi2[:], quads[:, :, 0, :], quads[:, :, 1, :], ALU.max)
-            return hi2, lo2
+            return members[:].rearrange("p t (j u v) -> p (t j) u v", u=2, v=2)
+
+        def pair(quads, op, name):
+            tile = ring.tile([P, quads.shape[1], 2], F32, name=name)
+            nc.vector.tensor_tensor(tile[:], quads[:, :, 0, :], quads[:, :, 1, :], op)
+            return tile
 
         def finish(pairs, op, name):
             tile = ring.tile([P, pairs.shape[1]], F32, name=name)
@@ -255,7 +268,8 @@ def tile_picked_twksjointbgspan_none_po_kernel(
                 nc.sync.dma_start(out_rows[:, :, out_starts[c] : out_starts[c] + OUT_CHUNKS[c]], ys[c][:])
 
         def group_y(c):
-            nc.vector.tensor_copy(
+            cast = nc.scalar.copy if c in SCALAR_GROUPS else nc.vector.tensor_copy
+            cast(
                 y_grouped[c][:].rearrange("p (c i) t -> p c t i", i=PACK), ys[c][:].rearrange("p t (c i) -> p c t i", i=PACK)
             )
 
@@ -266,19 +280,22 @@ def tile_picked_twksjointbgspan_none_po_kernel(
             )
             nc.sync.dma_start(out_wd[:, cols], y_wd[:, cols].bitcast(I32))
 
-        for u in range(len(halves) + 1):
+        for u in range(len(halves) + 3):
             if u < len(halves):
-                hi2, lo2 = fetch_and_pair(u)
-            if u >= 1:
+                quads = fetch(u)
+                lo2 = pair(quads, ALU.min, "lo2")
+            if u >= 4 and u % 2 == 0:
+                quantise_y(u // 2 - 2)
+            if u < len(halves):
+                hi2 = pair(quads, ALU.max, "hi2")
+            if 1 <= u <= len(halves):
                 combine(u - 1, top, low)
             if u < len(halves):
                 low = finish(lo2, ALU.min, "low")
-            if u >= 2 and u % 2 == 0:
+            if u >= 3 and u % 2 == 1:
                 group_y(u // 2 - 1)
             if u < len(halves):
                 top = finish(hi2, ALU.max, "top")
-            if u >= 2 and u % 2 == 0:
-                quantise_y(u // 2 - 1)
         for q in range(P // QUAD):
             queue = nc.sync if q % 2 == 0 else nc.scalar
             queue.dma_start(

@@ -49,6 +49,12 @@ def tile_picked_twksjointbgspan_none_po_kernel(
                 lo = QUAD * q
                 queue.dma_start(tile[lo : lo + PACK, :].bitcast(I32), dram[0, PACK * q : PACK * (q + 1), :].bitcast(I32))
 
+        def deal(copy, dealt, plain, run):
+            copy(dealt.rearrange("p t (c i) -> p c t i", i=run), plain.rearrange("p (c i t) -> p c t i", t=PACK, i=run))
+
+        def by_tile(ap):
+            return ap.rearrange("p (t m) -> p t m", t=PACK)
+
         def entries(tile, lo, count):
             return tile[:, lo // LANE : (lo + count) // LANE]
 
@@ -89,9 +95,7 @@ def tile_picked_twksjointbgspan_none_po_kernel(
         key_sc_got = keep.tile([P, H], U8, name="key_sc_got")
         nc.vector.tensor_copy(key_sc_got[:], d_sc[:].indirect(k1_t[:]))
         key_sc = keep.tile([P, H], U8, name="key_sc", align_bytes=64)
-        nc.vector.tensor_copy(
-            key_sc[:].rearrange("p (t m) -> p t m", t=PACK), key_sc_got[:].rearrange("p (m t) -> p t m", t=PACK)
-        )
+        deal(nc.vector.tensor_copy, by_tile(key_sc[:]), key_sc_got[:], 16)
         for r in range(1, PACK):
             nc.scalar.dma_start(key_sc[r:P:QUAD, :].bitcast(I32), key_sc[BLOCK * r : P : QUAD, :].bitcast(I32))
 
@@ -129,21 +133,13 @@ def tile_picked_twksjointbgspan_none_po_kernel(
             nc.vector.tensor_copy(got[:], d_wd[:].indirect(entries(k1_t, u * half, half)))
             gots.append(got)
         for u in range(2):
-            nc.vector.tensor_copy(
-                key_wd[:].rearrange("p (t m) -> p t m", t=PACK)[:, :, u * P // 2 : (u + 1) * P // 2],
-                gots[u][:].rearrange("p (m t) -> p t m", t=PACK),
-            )
+            deal(nc.vector.tensor_copy, by_tile(key_wd[:])[:, :, u * P // 2 : (u + 1) * P // 2], gots[u][:], 4)
         b_banks = scores(b_tokens, "b")
 
         w_wd = keep.tile([P, 2 * N], U8, name="w_wd", align_bytes=64)
-        nc.scalar.copy(
-            w_wd[:].bitcast(U16).rearrange("p (t m) -> p t m", t=PACK),
-            w_wd_raw[:].bitcast(U16).rearrange("p (m t) -> p t m", t=PACK),
-        )
+        deal(nc.scalar.copy, by_tile(w_wd[:].bitcast(U16)), w_wd_raw[:].bitcast(U16), 8)
         w_sc = keep.tile([P, N], U8, name="w_sc", align_bytes=64)
-        nc.gpsimd.tensor_copy(
-            w_sc[:].rearrange("p (t m) -> p t m", t=PACK), w_sc_raw[:].rearrange("p (m t) -> p t m", t=PACK)
-        )
+        deal(nc.gpsimd.tensor_copy, by_tile(w_sc[:]), w_sc_raw[:], 16)
 
         starts = [sum(Z_CHUNKS[:c]) for c in range(len(Z_CHUNKS))]
         units = [(c, t) for c in range(len(Z_CHUNKS)) for t in range(PACK)]
@@ -247,22 +243,22 @@ def tile_picked_twksjointbgspan_none_po_kernel(
                     nc.vector.tensor_copy(members[:, s, :], window)
                 else:
                     nc.scalar.activation(members[:, s, :], window, ACT.Copy)
-            return members[:].rearrange("p t (j u v) -> p (t j) u v", u=2, v=2)
+            return members[:].rearrange("p t (g i u v) -> p (t g) i u v", i=2, u=2, v=2)
 
         def pair(quads, op, name):
-            tile = ring.tile([P, quads.shape[1], 2], F32, name=name)
-            nc.vector.tensor_tensor(tile[:], quads[:, :, 0, :], quads[:, :, 1, :], op)
+            tile = ring.tile([P, quads.shape[1], 2, 2], F32, name=name)
+            nc.vector.tensor_tensor(tile[:].rearrange("p g v i -> p g i v"), quads[:, :, :, 0, :], quads[:, :, :, 1, :], op)
             return tile
 
         def finish(pairs, op, name):
-            tile = ring.tile([P, pairs.shape[1]], F32, name=name)
-            nc.vector.tensor_tensor(tile[:], pairs[:, :, 0], pairs[:, :, 1], op)
+            tile = ring.tile([P, pairs.shape[1], 2], F32, name=name)
+            nc.vector.tensor_tensor(tile[:], pairs[:, :, 0, :], pairs[:, :, 1, :], op)
             return tile
 
         def combine(u, top, low):
             c, half = halves[u]
             nc.vector.scalar_tensor_tensor(
-                ys[c][:, 2 * half : 2 * half + 2, :].rearrange("p t j -> p (t j)"), low[:], -0.5, top[:], ALU.mult, ALU.add
+                ys[c][:, 2 * half : 2 * half + 2, :].rearrange("p t j -> p (t j)"), low[:].rearrange("p g i -> p (g i)"), -0.5, top[:].rearrange("p g i -> p (g i)"), ALU.mult, ALU.add
             )
             if half == 1:
                 nc.sync.dma_start(out_rows[:, :, out_starts[c] : out_starts[c] + OUT_CHUNKS[c]], ys[c][:])

from contextlib import ExitStack

import concourse.mybir as mybir

K, T, S, N, G, H = 512, 2048, 512, 512, 2048, 512
FLOPS = 2 * K * H * S * 2 + 2 * H * N * S

F32 = mybir.dt.float32
BF16 = mybir.dt.bfloat16
I32 = mybir.dt.int32
U32 = mybir.dt.uint32
U16 = mybir.dt.uint16
U8 = mybir.dt.uint8
FP8X4 = mybir.dt.float8_e4m3fn_x4
FP4X4 = mybir.dt.float4_e2m1fn_x4
ALU = mybir.AluOpType
ACT = mybir.ActivationFunctionType

P = 128
PACK = 4
LANE = 16
QUAD = 32
BLOCK = 8
SPARE = 32
SCORE_SCALE = 0.0625
Z_CHUNKS = (256, 256)
OUT_CHUNKS = (64, 128, 128, 128, 64)
SCALAR_GROUPS = (3,)
VECTOR_FETCHES = ((0, 1), (0, 3), (1, 1))


def tile_picked_twksjointbgspan_none_po_kernel(
    tc, x_words, x_scales, d_words, d_scales, gn, w1_words, w1_scales, offs, k1, two, n1, n2, n3, out_0, out_1, out_2
):
    nc = tc.nc
    with ExitStack() as ctx:
        lists = ctx.enter_context(tc.tile_pool(name="lists", bufs=1))
        keep = ctx.enter_context(tc.tile_pool(name="keep", bufs=1))
        ring = ctx.enter_context(tc.tile_pool(name="ring", bufs=3))
        psum = ctx.enter_context(tc.psum_pool(name="psum", bufs=1))

        def load_list(dram, name):
            tile = lists.tile(list(dram.shape), U16, name=name)
            nc.sync.dma_start(tile[:], dram)
            return tile

        def load_scale_rows(queue, tile, dram):
            for q in range(P // QUAD):
                lo = QUAD * q
                queue.dma_start(tile[lo : lo + PACK, :].bitcast(I32), dram[0, PACK * q : PACK * (q + 1), :].bitcast(I32))

        def deal(copy, dealt, plain, run):
            copy(dealt.rearrange("p t (c i) -> p c t i", i=run), plain.rearrange("p (c i t) -> p c t i", t=PACK, i=run))

        def by_tile(ap):
            return ap.rearrange("p (t m) -> p t m", t=PACK)

        def entries(tile, lo, count):
            return tile[:, lo // LANE : (lo + count) // LANE]

        x_sc = keep.tile([P, T], U8, name="x_sc")
        w_sc_raw = keep.tile([P, N], U8, name="w_sc_raw")
        nc.vector.memset(x_sc[:].bitcast(I32), 0)
        nc.gpsimd.memset(w_sc_raw[:].bitcast(I32), 0)
        z_sc = [keep.tile([P, w], U8, name=f"z_sc{c}", align_bytes=64) for c, w in enumerate(Z_CHUNKS)]
        for tile in z_sc:
            nc.vector.memset(tile[:].bitcast(I32), 0)
        h_rows = [keep.tile([P, S + SPARE], F32, name=f"h_row{t}") for t in range(PACK)]
        for tile in h_rows:
            nc.vector.memset(tile[:, S:], 0.0)

        d_sc = keep.tile([P, G], U8, name="d_sc")
        d_wd = keep.tile([P, G], U32, name="d_wd")
        x_wd = keep.tile([P, T], U32, name="x_wd")
        k1_t = load_list(k1, "k1_t")
        two_t = load_list(two, "two_t")
        nc.sync.dma_start(
            d_sc[:].bitcast(I32), d_scales[0].bitcast(I32).unsqueeze(1).broadcast_to([K // QUAD, BLOCK, G // PACK])
        )
        nc.sync.dma_start(x_wd[:].bitcast(I32), x_words[0].rearrange("p n t -> p (n t)").bitcast(I32))
        nc.sync.dma_start(d_wd[:].bitcast(I32), d_words[0].rearrange("p n t -> p (n t)").bitcast(I32))
        load_scale_rows(nc.scalar, x_sc, x_scales)
        offs_t = load_list(offs, "offs_t")
        n1_t = load_list(n1, "n1_t")
        n2_t = load_list(n2, "n2_t")
        n3_t = load_list(n3, "n3_t")
        gn_t = keep.tile([P, PACK], F32, name="gn_t")
        nc.gpsimd.dma_start(gn_t[:], gn.rearrange("(p t) o -> p (t o)", t=PACK))
        w_wd_raw = keep.tile([P, 2 * N], U8, name="w_wd_raw")
        nc.gpsimd.dma_start(w_wd_raw[:].bitcast(I32), w1_words[0].bitcast(I32))
        load_scale_rows(nc.gpsimd, w_sc_raw, w1_scales)
        gain = keep.tile([P, PACK], F32, name="gain")
        nc.scalar.activation(gain[:], gn_t[:], ACT.Copy, scale=SCORE_SCALE)

        key_sc_got = keep.tile([P, H], U8, name="key_sc_got")
        nc.vector.tensor_copy(key_sc_got[:], d_sc[:].indirect(k1_t[:]))
        key_sc = keep.tile([P, H], U8, name="key_sc", align_bytes=64)
        deal(nc.vector.tensor_copy, by_tile(key_sc[:]), key_sc_got[:], 16)
        for r in range(1, PACK):
            nc.scalar.dma_start(key_sc[r:P:QUAD, :].bitcast(I32), key_sc[BLOCK * r : P : QUAD, :].bitcast(I32))

        def pick_tokens(list_t, name, tags):
            tok_wd = keep.tile([P, S], U32, name=name + "_wd", tag=tags[1], align_bytes=64)
            nc.vector.tensor_copy(tok_wd[:], x_wd[:].indirect(list_t[:]))
            tok_sc = keep.tile([P, S], U8, name=name + "_sc", tag=tags[0], align_bytes=64)
            nc.vector.tensor_copy(tok_sc[:], x_sc[:].indirect(list_t[:]))
            return tok_wd, tok_sc

        def scores(tokens, name):
            tok_wd, tok_sc = tokens
            banks = []
            for t in range(PACK):
                bank = psum.tile([P, S], F32, name=f"{name}{t}", tag=f"{name}{t}")
                cols = slice(t * P, (t + 1) * P)
                nc.tensor.matmul_mx(
                    out=bank[:],
                    lhsT=key_wd[:, cols].bitcast(FP8X4),
                    lhsT_scale=key_sc[:, cols],
                    rhs=tok_wd[:].bitcast(FP8X4),
                    rhs_scale=tok_sc[:],
                    start=True,
                    stop=True,
                )
                banks.append(bank)
            return banks

        b_tokens = pick_tokens(two_t, "b", ("b_sc", "b_wd"))
        key_wd = keep.tile([P, H], U32, name="key_wd", align_bytes=64)
        half = H // 2
        gots = []
        for u in range(2):
            got = keep.tile([P, half], U32, name=f"key_wd_got{u}", tag=f"staged{u}", align_bytes=64)
            nc.vector.tensor_copy(got[:], d_wd[:].indirect(entries(k1_t, u * half, half)))
            gots.append(got)
        for u in range(2):
            deal(nc.vector.tensor_copy, by_tile(key_wd[:])[:, :, u * P // 2 : (u + 1) * P // 2], gots[u][:], 4)
        b_banks = scores(b_tokens, "b")

        w_wd = keep.tile([P, 2 * N], U8, name="w_wd", align_bytes=64)
        deal(nc.scalar.copy, by_tile(w_wd[:].bitcast(U16)), w_wd_raw[:].bitcast(U16), 8)
        w_sc = keep.tile([P, N], U8, name="w_sc", align_bytes=64)
        deal(nc.gpsimd.tensor_copy, by_tile(w_sc[:]), w_sc_raw[:], 16)

        starts = [sum(Z_CHUNKS[:c]) for c in range(len(Z_CHUNKS))]
        units = [(c, t) for c in range(len(Z_CHUNKS)) for t in range(PACK)]
        b_rows = [keep.tile([P, S], F32, name=f"b_row{t}") for t in range(PACK)]
        first = [keep.tile([P, Z_CHUNKS[c]], F32, name=f"first{c}{t}") for c, t in units]
        diff = [keep.tile([P, Z_CHUNKS[c]], F32, name=f"diff{c}{t}") for c, t in units]
        gate = [keep.tile([P, Z_CHUNKS[c]], F32, name=f"gate{c}{t}") for c, t in units]
        z_planes = [keep.tile([P, PACK, w], BF16, name=f"z_planes{c}") for c, w in enumerate(Z_CHUNKS)]
        z_grouped = [keep.tile([P, w, PACK], BF16, name=f"z_grouped{c}", align_bytes=64) for c, w in enumerate(Z_CHUNKS)]
        z_wd = [keep.tile([P, w], U32, name=f"z_wd{c}", align_bytes=64) for c, w in enumerate(Z_CHUNKS)]

        def fetch_first(u):
            c, t = units[u]
            nc.scalar.activation(first[u][:], b_rows[t][:].indirect(entries(n1_t, starts[c], Z_CHUNKS[c])), ACT.Copy)

        def fetch_second(u):
            c, t = units[u]
            nc.vector.tensor_tensor(
                diff[u][:], b_rows[t][:].indirect(entries(n2_t, starts[c], Z_CHUNKS[c])), first[u][:], ALU.subtract
            )

        def squash(u):
            nc.scalar.activation(gate[u][:], diff[u][:], ACT.Tanh, scale=-SCORE_SCALE)

        def apply_gate(u):
            c, t = units[u]
            cols = slice(starts[c], starts[c] + Z_CHUNKS[c])
            nc.vector.scalar_tensor_tensor(
                z_planes[c][:, t, :], a_banks[t][:, cols], gain[:, t : t + 1], gate[u][:], ALU.mult, ALU.mult
            )

        def group_z(c):
            nc.vector.tensor_copy(
                z_grouped[c][:].rearrange("p (c i) t -> p c t i", i=PACK),
                z_planes[c][:].rearrange("p t (c i) -> p c t i", i=PACK),
            )

        def layer(c):
            width = Z_CHUNKS[c]
            nc.vector.quantize_mx(
                out=z_wd[c][:].bitcast(FP8X4), scales=z_sc[c][:], in_=z_grouped[c][:].rearrange("p w t -> p (w t)")
            )
            last = c == len(Z_CHUNKS) - 1
            per_bank = 1 if last else S // width
            for t in range(PACK):
                if t % per_bank == 0:
                    tag = f"a{t}" if last else f"b{(PACK * starts[c] + t * width) // S}"
                    h_bank = psum.tile([P, S], F32, name=f"h{c}{t}", tag=tag)
                slot = slice((t % per_bank) * width, (t % per_bank + 1) * width)
                nc.tensor.matmul_mx(
                    out=h_bank[:, slot],
                    lhsT=w_wd[:, 2 * t * P : 2 * (t + 1) * P].bitcast(FP4X4),
                    lhsT_scale=w_sc[:, t * P : (t + 1) * P],
                    rhs=z_wd[c][:].bitcast(FP8X4),
                    rhs_scale=z_sc[c][:],
                    start=True,
                    stop=True,
                )
                if t % per_bank == per_bank - 1:
                    for s in range(per_bank):
                        row = h_rows[t + 1 - per_bank + s][:, starts[c] : starts[c] + width]
                        if last and t % 2 == 1:
                            nc.vector.tensor_copy(row, h_bank[:, s * width : (s + 1) * width])
                        else:
                            nc.scalar.copy(row, h_bank[:, s * width : (s + 1) * width])

        for t in range(PACK):
            nc.scalar.copy(b_rows[t][:], b_banks[t][:])
            fetch_first(t)
        a_banks = scores(pick_tokens(offs_t, "a", ("staged0", "staged1")), "a")
        for step in range(len(units) + 4):
            if step < len(units):
                fetch_second(step)
            if step + PACK < len(units):
                fetch_first(step + PACK)
            if 1 <= step <= len(units):
                squash(step - 1)
            if 2 <= step <= len(units) + 1:
                apply_gate(step - 2)
            if step >= PACK + 2 and (step - 2) % PACK == 0:
                group_z((step - 2) // PACK - 1)
            if step >= PACK + 3 and (step - 3) % PACK == 0:
                layer((step - 3) // PACK - 1)

        y_wd = keep.tile([P, S], U32, name="y_wd", align_bytes=64)
        y_sc = keep.tile([P, S], U8, name="y_sc", align_bytes=64)
        out_rows = out_0.rearrange("(p t) j -> p t j", t=PACK)
        out_wd = out_1[0].rearrange("p n t -> p (n t)").bitcast(I32)
        out_starts = [sum(OUT_CHUNKS[:c]) for c in range(len(OUT_CHUNKS))]
        halves = [(c, half) for c in range(len(OUT_CHUNKS)) for half in range(2)]
        ys = [keep.tile([P, PACK, w], F32, name=f"y{c}") for c, w in enumerate(OUT_CHUNKS)]
        y_grouped = [keep.tile([P, w, PACK], BF16, name=f"y_grouped{c}", align_bytes=64) for c, w in enumerate(OUT_CHUNKS)]

        def fetch(u):
            c, half = halves[u]
            picks = PACK * OUT_CHUNKS[c]
            members = ring.tile([P, 2, picks], F32, name="members", bufs=4)
            for s in range(2):
                window = h_rows[2 * half + s][:].indirect(entries(n3_t, PACK * out_starts[c], picks))
                if (c, 2 * half + s) in VECTOR_FETCHES:
                    nc.vector.tensor_copy(members[:, s, :], window)
                else:
                    nc.scalar.activation(members[:, s, :], window, ACT.Copy)
            return members[:].rearrange("p t (g i u v) -> p (t g) i u v", i=2, u=2, v=2)

        def pair(quads, op, name):
            tile = ring.tile([P, quads.shape[1], 2, 2], F32, name=name)
            nc.vector.tensor_tensor(tile[:].rearrange("p g v i -> p g i v"), quads[:, :, :, 0, :], quads[:, :, :, 1, :], op)
            return tile

        def finish(pairs, op, name):
            tile = ring.tile([P, pairs.shape[1], 2], F32, name=name)
            nc.vector.tensor_tensor(tile[:], pairs[:, :, 0, :], pairs[:, :, 1, :], op)
            return tile

        def combine(u, top, low):
            c, half = halves[u]
            nc.vector.scalar_tensor_tensor(
                ys[c][:, 2 * half : 2 * half + 2, :].rearrange("p t j -> p (t j)"), low[:].rearrange("p g i -> p (g i)"), -0.5, top[:].rearrange("p g i -> p (g i)"), ALU.mult, ALU.add
            )
            if half == 1:
                nc.sync.dma_start(out_rows[:, :, out_starts[c] : out_starts[c] + OUT_CHUNKS[c]], ys[c][:])

        def group_y(c):
            cast = nc.scalar.copy if c in SCALAR_GROUPS else nc.vector.tensor_copy
            cast(
                y_grouped[c][:].rearrange("p (c i) t -> p c t i", i=PACK), ys[c][:].rearrange("p t (c i) -> p c t i", i=PACK)
            )

        def quantise_y(c):
            cols = slice(out_starts[c], out_starts[c] + OUT_CHUNKS[c])
            nc.vector.quantize_mx(
                out=y_wd[:, cols].bitcast(FP8X4), scales=y_sc[:, cols], in_=y_grouped[c][:].rearrange("p w t -> p (w t)")
            )
            nc.sync.dma_start(out_wd[:, cols], y_wd[:, cols].bitcast(I32))

        for u in range(len(halves) + 3):
            if u < len(halves):
                quads = fetch(u)
                lo2 = pair(quads, ALU.min, "lo2")
            if u >= 4 and u % 2 == 0:
                quantise_y(u // 2 - 2)
            if u < len(halves):
                hi2 = pair(quads, ALU.max, "hi2")
            if 1 <= u <= len(halves):
                combine(u - 1, top, low)
            if u < len(halves):
                low = finish(lo2, ALU.min, "low")
            if u >= 3 and u % 2 == 1:
                group_y(u // 2 - 1)
            if u < len(halves):
                top = finish(hi2, ALU.max, "top")
        for q in range(P // QUAD):
            queue = nc.sync if q % 2 == 0 else nc.scalar
            queue.dma_start(
                out_2[0, PACK * q : PACK * (q + 1), :].bitcast(I32), y_sc[QUAD * q : QUAD * q + PACK, :].bitcast(I32)
            )
